import numpy as np
import ml_dtypes


def mxq(x, axis, fmt="e4m3"):
    dtype, down = {"e4m3": (ml_dtypes.float8_e4m3fn, 7), "e5m2": (ml_dtypes.float8_e5m2, 14)}[fmt]
    v = np.moveaxis(np.asarray(x, np.float32).astype(ml_dtypes.bfloat16).astype(np.float64), axis, -1)
    blocks = v.reshape(v.shape[:-1] + (-1, 32))
    amax = np.abs(blocks).max(-1, keepdims=True)
    byte = np.maximum(np.where(amax > 0, np.frexp(amax)[1] - 1 + 127, 0) - down, 1)
    scale = np.exp2(byte - 127.0)
    codes = (blocks / scale).astype(np.float32).astype(dtype).astype(np.float64)
    return np.moveaxis((codes * scale).reshape(v.shape), -1, axis)


WIDE = False


def mx_kscale(k):
    if not WIDE:
        return np.ones(k)
    levels = np.array([10, -10, 5, -5, 0])
    if k % 512:
        return np.exp2(np.random.permutation(np.resize(levels, k // 32))).repeat(32)
    a = np.empty((k // 512, 16))
    for p in range(k // 512):
        a[p, :8] = np.random.permutation(np.resize(levels, 8))
        for g in range(8):
            far = levels[np.abs(levels - a[p, g]) >= 10]
            a[p, g + 8] = far[np.random.randint(len(far))]
    return np.exp2(a.ravel()).repeat(32)


def f64(x):
    return np.asarray(x).astype(np.float64)


def striped(idx):
    return np.tile(np.asarray(idx).reshape(-1, 16).T, (8, 1)).astype(np.uint16)


def unstriped(offs):
    return offs[:16].T.reshape(-1).astype(np.int64)


B, N, T, D, NQ = 2, 512, 2048, 512, 128


def setup_inputs():
    n = np.random.standard_normal
    jdx = np.random.permutation(1024)[:B * NQ]
    pages = np.random.permutation(T // 64)[:B * N // 64]
    idx = (pages[:, None] * 64 + np.arange(64)[None, :]).reshape(-1)
    s = mx_kscale(D)[:, None]
    return {
        "qT": (n((D, 1024)) * s * (1.00 / np.sqrt(D))).astype(np.float32),
        "kT": (n((D, T)) / s).astype(np.float32),
        "offq": striped(jdx),
        "offs": striped(idx),
    }


def reference(qT, kT, offq, offs):
    jdx = unstriped(offq)
    idx = unstriped(offs)
    pick = lambda x, which: x[:, which].reshape(x.shape[0], B, -1).transpose(1, 0, 2)
    qg = mxq(pick(f64(qT), jdx), 1, "e4m3")
    kg = mxq(pick(f64(kT), idx), 1, "e4m3")
    qq = qg
    a = qq.transpose(0, 2, 1) @ kg
    return a

import concourse.mybir as mybir

B, N, T, D, NQ, TQ = 2, 512, 2048, 512, 128, 1024
FLOPS = 2 * B * NQ * N * D

F32 = mybir.dt.float32
BF16 = mybir.dt.bfloat16
U32 = mybir.dt.uint32
U16 = mybir.dt.uint16
U8 = mybir.dt.uint8
FP8X4 = mybir.dt.float8_e4m3fn_x4

P = 128
PACK = 4
PIECE = 256
PIECES = B * N // PIECE


def tile_attend_both_f_kernel(tc, qT, kT, offq, offs, out):
    nc = tc.nc
    k_planes = kT.rearrange("(p t) n -> p t n", t=PACK)
    q_planes = qT.rearrange("(p t) n -> p t n", t=PACK)
    with (
        tc.tile_pool(name="keep", bufs=1) as keep,
        tc.psum_pool(name="psum", bufs=1) as psum,
    ):
        k_list = keep.tile([P, B * N // 16], U16, name="k_list")
        q_list = keep.tile([P, B * NQ // 16], U16, name="q_list")
        k_pool = [keep.tile([P, T], F32, name=f"k_pool{t}") for t in range(PACK)]
        q_pool = [keep.tile([P, TQ], F32, name=f"q_pool{t}") for t in range(PACK)]

        nc.sync.dma_start(k_pool[0][:], k_planes[:, 0, :])
        nc.sync.dma_start(k_list[:], offs)
        nc.sync.dma_start(q_list[:], offq)
        for t in range(1, PACK):
            nc.sync.dma_start(k_pool[t][:], k_planes[:, t, :])
        for t in range(PACK):
            nc.sync.dma_start(q_pool[t][:], q_planes[:, t, :])

        k_pair = [[keep.tile([P, 2, PIECE], F32, name=f"k_pair{u}_{j}") for j in range(PIECES)] for u in range(2)]
        k_bf = [keep.tile([P, PIECE, PACK], BF16, name=f"k_bf{j}", align_bytes=64) for j in range(PIECES)]
        k_codes = [keep.tile([P, PIECE], U32, name=f"k_codes{j}", align_bytes=64) for j in range(PIECES)]
        k_scales = [keep.tile([P, PIECE], U8, name=f"k_scales{j}", align_bytes=64) for j in range(PIECES)]
        q_pair = keep.tile([P, 2, B * NQ], F32, name="q_pair")
        q_bf = [keep.tile([P, NQ, PACK], BF16, name=f"q_bf{b}", align_bytes=64) for b in range(B)]
        q_codes = [keep.tile([P, NQ], U32, name=f"q_codes{b}", align_bytes=64) for b in range(B)]
        q_scales = [keep.tile([P, NQ], U8, name=f"q_scales{b}", align_bytes=64) for b in range(B)]

        def gather_k(t, j):
            cols = PIECE // 16
            nc.vector.tensor_copy(k_pair[t // 2][j][:, t % 2, :], k_pool[t][:].indirect(k_list[:, j * cols:(j + 1) * cols]))

        def pair_k(engine_copy, u, j):
            engine_copy(k_bf[j][:, :, 2 * u:2 * u + 2], k_pair[u][j][:].rearrange("p e n -> p n e"))

        def quantize(codes, scales, values):
            nc.vector.quantize_mx(out=codes[:].bitcast(FP8X4), scales=scales[:], in_=values[:].rearrange("p n t -> p (n t)"))

        def gather_q_pair(t):
            nc.vector.tensor_copy(q_pair[:, t, :], q_pool[t][:].indirect(q_list[:]))

        def gather_q_step(t, b):
            cols = NQ // 16
            nc.vector.tensor_copy(q_bf[b][:, :, t], q_pool[t][:].indirect(q_list[:, b * cols:(b + 1) * cols]))

        for j in range(PIECES):
            gather_k(0, j)
        for j in range(PIECES):
            gather_k(1, j)
            if j < 2:
                pair_k(nc.scalar.copy, 0, j)
        for j in range(2, PIECES):
            pair_k(nc.vector.tensor_copy, 0, j)
        for j in range(PIECES):
            gather_k(2, j)
        for j in range(PIECES):
            gather_k(3, j)
            pair_k(nc.scalar.copy, 1, j)
        gather_q_pair(0)
        quantize(k_codes[0], k_scales[0], k_bf[0])
        quantize(k_codes[1], k_scales[1], k_bf[1])
        gather_q_pair(1)
        for b in range(B):
            nc.scalar.copy(q_bf[b][:, :, 0:2], q_pair[:, :, b * NQ:(b + 1) * NQ].rearrange("p e n -> p n e"))
        quantize(k_codes[2], k_scales[2], k_bf[2])
        for b in range(B):
            gather_q_step(2, b)
        quantize(k_codes[3], k_scales[3], k_bf[3])
        for b in range(B):
            gather_q_step(3, b)
        for b in range(B):
            quantize(q_codes[b], q_scales[b], q_bf[b])

        for j in range(PIECES):
            b, h = divmod(j, N // PIECE)
            acc = psum.tile([NQ, PIECE], F32, name=f"acc{j}")
            nc.tensor.matmul_mx(out=acc[:], lhsT=q_codes[b][:].bitcast(FP8X4), lhsT_scale=q_scales[b][:],
                                rhs=k_codes[j][:].bitcast(FP8X4), rhs_scale=k_scales[j][:], start=True, stop=True)
            res = keep.tile([NQ, PIECE], F32, name=f"res{j}")
            if j % 2 == 0:
                nc.scalar.copy(res[:], acc[:])
            else:
                nc.vector.tensor_copy(res[:], acc[:])
            nc.sync.dma_start(out[b, :, h * PIECE:(h + 1) * PIECE], res[:])
